import numpy as np
import ml_dtypes

BF16 = ml_dtypes.bfloat16


def bf(x):
    return np.asarray(x, np.float32).astype(BF16)


def f32(x):
    return np.asarray(x, np.float32)


def f64(x):
    return np.asarray(x).astype(np.float64)


def striped(idx):
    return np.tile(idx.reshape(-1, 16).T, (8, 1))


S, K, M, N, B, Q = 512, 512, 128, 384, 4, 96


def setup_inputs():
    return {"base": bf(np.random.standard_normal((B, M, S))), "x": bf(np.random.standard_normal((K, N))), "w": bf(np.random.standard_normal((K, M)) / np.sqrt(K)), "b": f32(0.5 * np.random.standard_normal((M, 1))), "offs": striped(np.random.permutation(S)[:N])}


def reference(base, x, w, b, offs):
    idx = offs[:16].T.reshape(-1)
    z = f64(base).copy()
    for i in range(B):
        z[i][:, idx[i * Q : (i + 1) * Q]] += f64(w).T @ f64(x)[:, i * Q : (i + 1) * Q]
    return np.maximum(z + f64(b), 0.0)

@@ -1,0 +1,65 @@
+import concourse.mybir as mybir
+from concourse.masks import make_identity
+
+BF16, F32, U16 = mybir.dt.bfloat16, mybir.dt.float32, mybir.dt.uint16
+RELU = mybir.ActivationFunctionType.Relu
+ADD, MAX = mybir.AluOpType.add, mybir.AluOpType.max
+
+P = 128
+B, S = 4, 512
+K, N = 512, 384
+KB = K // P
+Q = N // B
+QC = Q // 16
+
+FLOPS = 2 * K * P * N
+
+
+def tile_scatter_matmul_kernel(tc, base, x, w, b, offs, out):
+    nc = tc.nc
+    with (
+        tc.tile_pool(name="held", bufs=1) as held,
+        tc.psum_pool(name="banks", bufs=1) as banks,
+    ):
+        offsets = held.tile([P, N // 16], U16, name="offsets")
+        nc.sync.dma_start(offsets[:], offs)
+
+        ident = held.tile([P, P], BF16, name="ident")
+        make_identity(nc, ident[:])
+
+        base_tiles = [held.tile([P, S], BF16, name=f"base{i}") for i in range(B)]
+        for i in range(B):
+            queue = nc.sync if i % 2 == 0 else nc.scalar
+            queue.dma_start(base_tiles[i][:], base[i])
+
+        w_tile = held.tile([P, KB, P], BF16, name="w_tile")
+        nc.sync.dma_start(w_tile[:], w.rearrange("(kb p) m -> p kb m", p=P))
+        x_tile = held.tile([P, KB, N], BF16, name="x_tile")
+        nc.scalar.dma_start(x_tile[:], x.rearrange("(kb p) n -> p kb n", p=P))
+
+        bias = held.tile([P, 1], F32, name="bias")
+        nc.sync.dma_start(bias[:], b)
+
+        windows = [banks.tile([P, S], F32, name=f"window{i}") for i in range(B)]
+        for i in range(B):
+            nc.tensor.matmul(windows[i][:], ident[:], base_tiles[i][:], start=True, stop=False)
+
+        for i in range(B):
+            piece = offsets[:, i * QC : (i + 1) * QC]
+            for kb in range(KB):
+                nc.tensor.matmul(
+                    windows[i][:].indirect(piece),
+                    w_tile[:, kb, :],
+                    x_tile[:, kb, i * Q : (i + 1) * Q],
+                    start=False,
+                    stop=(kb == KB - 1),
+                )
+
+        for i in range(B):
+            result = held.tile([P, S], F32, name=f"result{i}")
+            if i % 2 == 0:
+                nc.scalar.activation(result[:], windows[i][:], RELU, bias=bias[:, 0:1])
+                nc.scalar.dma_start(out[i], result[:])
+            else:
+                nc.vector.tensor_scalar(result[:], windows[i][:], bias[:, 0:1], 0.0, ADD, MAX)
+                nc.sync.dma_start(out[i], result[:])

@@ -13,6 +13,9 @@ Q = N // B
 QC = Q // 16
 
 FLOPS = 2 * K * P * N
+G = 2
+KH = KB // G
+WARM = 3
 
 
 def tile_scatter_matmul_kernel(tc, base, x, w, b, offs, out):
@@ -24,42 +27,53 @@ def tile_scatter_matmul_kernel(tc, base, x, w, b, offs, out):
         offsets = held.tile([P, N // 16], U16, name="offsets")
         nc.sync.dma_start(offsets[:], offs)
 
+        bias = held.tile([P, 1], F32, name="bias")
+        nc.scalar.dma_start(bias[:], b)
+
+        base_pairs = [held.tile([P, G, S], BF16, name=f"base_pair{g}") for g in range(B // G)]
+        for g, queue in enumerate((nc.sync, nc.scalar)):
+            queue.dma_start(base_pairs[g][:], base[g * G : (g + 1) * G].rearrange("i m t -> m i t"))
+
+        w_tile = held.tile([P, KB, P], BF16, name="w_tile")
+        nc.scalar.dma_start(w_tile[:], w.rearrange("(p kb) m -> p kb m", kb=KB))
+        x_rows = x.rearrange("(p kb) n -> p kb n", kb=KB)
+        x_halves = [held.tile([P, KH, N], BF16, name=f"x_half{h}") for h in range(G)]
+        for h, queue in enumerate((nc.sync, nc.scalar)):
+            queue.dma_start(x_halves[h][:], x_rows[:, h * KH : (h + 1) * KH, :])
+
+        zeros = held.tile([P, S], BF16, name="zeros")
+        nc.vector.memset(zeros[:], 0.0)
+        unused_bank = banks.tile([P, S], F32, name="unused_bank")
+        for r in range(WARM):
+            nc.tensor.matmul(unused_bank[:], zeros[:, 0:P], zeros[:], start=True, stop=True)
+        unused_relu = held.tile([P, 1], F32, name="unused_relu")
+        nc.scalar.activation(unused_relu[:], zeros[:, 0:1], RELU)
+
         ident = held.tile([P, P], BF16, name="ident")
         make_identity(nc, ident[:])
 
-        base_tiles = [held.tile([P, S], BF16, name=f"base{i}") for i in range(B)]
-        for i in range(B):
-            queue = nc.sync if i % 2 == 0 else nc.scalar
-            queue.dma_start(base_tiles[i][:], base[i])
-
-        w_tile = held.tile([P, KB, P], BF16, name="w_tile")
-        nc.sync.dma_start(w_tile[:], w.rearrange("(kb p) m -> p kb m", p=P))
-        x_tile = held.tile([P, KB, N], BF16, name="x_tile")
-        nc.scalar.dma_start(x_tile[:], x.rearrange("(kb p) n -> p kb n", p=P))
-
-        bias = held.tile([P, 1], F32, name="bias")
-        nc.sync.dma_start(bias[:], b)
-
         windows = [banks.tile([P, S], F32, name=f"window{i}") for i in range(B)]
         for i in range(B):
-            nc.tensor.matmul(windows[i][:], ident[:], base_tiles[i][:], start=True, stop=False)
+            nc.tensor.matmul(windows[i][:], ident[:], base_pairs[i // G][:, i % G, :], start=True, stop=False)
 
-        for i in range(B):
-            piece = offsets[:, i * QC : (i + 1) * QC]
-            for kb in range(KB):
-                nc.tensor.matmul(
-                    windows[i][:].indirect(piece),
-                    w_tile[:, kb, :],
-                    x_tile[:, kb, i * Q : (i + 1) * Q],
-                    start=False,
-                    stop=(kb == KB - 1),
-                )
+        for g in range(B // G):
+            for h in range(G):
+                for i in range(g * G, (g + 1) * G):
+                    for kh in range(KH):
+                        kb = h * KH + kh
+                        nc.tensor.matmul(
+                            windows[i][:].indirect(offsets[:, i * QC : (i + 1) * QC]),
+                            w_tile[:, kb, :],
+                            x_halves[h][:, kh, i * Q : (i + 1) * Q],
+                            start=False,
+                            stop=(kb == KB - 1),
+                        )
 
         for i in range(B):
             result = held.tile([P, S], F32, name=f"result{i}")
             if i % 2 == 0:
-                nc.scalar.activation(result[:], windows[i][:], RELU, bias=bias[:, 0:1])
-                nc.scalar.dma_start(out[i], result[:])
-            else:
                 nc.vector.tensor_scalar(result[:], windows[i][:], bias[:, 0:1], 0.0, ADD, MAX)
                 nc.sync.dma_start(out[i], result[:])
+            else:
+                nc.scalar.activation(result[:], windows[i][:], RELU, bias=bias[:, 0:1])
+                nc.scalar.dma_start(out[i], result[:])

@@ -15,7 +15,8 @@ QC = Q // 16
 FLOPS = 2 * K * P * N
 G = 2
 KH = KB // G
-WARM = 3
+C = 2
+WARM = 2
 
 
 def tile_scatter_matmul_kernel(tc, base, x, w, b, offs, out):
@@ -24,22 +25,19 @@ def tile_scatter_matmul_kernel(tc, base, x, w, b, offs, out):
         tc.tile_pool(name="held", bufs=1) as held,
         tc.psum_pool(name="banks", bufs=1) as banks,
     ):
-        offsets = held.tile([P, N // 16], U16, name="offsets")
-        nc.sync.dma_start(offsets[:], offs)
-
-        bias = held.tile([P, 1], F32, name="bias")
-        nc.scalar.dma_start(bias[:], b)
-
-        base_pairs = [held.tile([P, G, S], BF16, name=f"base_pair{g}") for g in range(B // G)]
-        for g, queue in enumerate((nc.sync, nc.scalar)):
-            queue.dma_start(base_pairs[g][:], base[g * G : (g + 1) * G].rearrange("i m t -> m i t"))
+        base_tiles = [held.tile([P, S], BF16, name=f"base{i}") for i in range(B)]
+        for i in range(B):
+            nc.sync.dma_start(base_tiles[i][:], base[i])
 
         w_tile = held.tile([P, KB, P], BF16, name="w_tile")
-        nc.scalar.dma_start(w_tile[:], w.rearrange("(p kb) m -> p kb m", kb=KB))
+        nc.sync.dma_start(w_tile[:], w.rearrange("(p kb) m -> p kb m", kb=KB))
         x_rows = x.rearrange("(p kb) n -> p kb n", kb=KB)
         x_halves = [held.tile([P, KH, N], BF16, name=f"x_half{h}") for h in range(G)]
-        for h, queue in enumerate((nc.sync, nc.scalar)):
-            queue.dma_start(x_halves[h][:], x_rows[:, h * KH : (h + 1) * KH, :])
+        nc.sync.dma_start(x_halves[0][:], x_rows[:, 0:KH, :])
+
+        offsets = held.tile([P, N // 16], U16, name="offsets")
+        nc.sync.dma_start(offsets[:], offs)
+        nc.sync.dma_start(x_halves[1][:], x_rows[:, KH:KB, :])
 
         zeros = held.tile([P, S], BF16, name="zeros")
         nc.vector.memset(zeros[:], 0.0)
@@ -52,28 +50,30 @@ def tile_scatter_matmul_kernel(tc, base, x, w, b, offs, out):
         ident = held.tile([P, P], BF16, name="ident")
         make_identity(nc, ident[:])
 
+        bias = held.tile([P, 1], F32, name="bias")
+        nc.gpsimd.dma_start(bias[:], b)
+
         windows = [banks.tile([P, S], F32, name=f"window{i}") for i in range(B)]
         for i in range(B):
-            nc.tensor.matmul(windows[i][:], ident[:], base_pairs[i // G][:, i % G, :], start=True, stop=False)
-
-        for g in range(B // G):
-            for h in range(G):
-                for i in range(g * G, (g + 1) * G):
-                    for kh in range(KH):
-                        kb = h * KH + kh
-                        nc.tensor.matmul(
-                            windows[i][:].indirect(offsets[:, i * QC : (i + 1) * QC]),
-                            w_tile[:, kb, :],
-                            x_halves[h][:, kh, i * Q : (i + 1) * Q],
-                            start=False,
-                            stop=(kb == KB - 1),
-                        )
+            nc.tensor.matmul(windows[i][:], ident[:], base_tiles[i][:], start=True, stop=False)
 
         for i in range(B):
-            result = held.tile([P, S], F32, name=f"result{i}")
-            if i % 2 == 0:
-                nc.vector.tensor_scalar(result[:], windows[i][:], bias[:, 0:1], 0.0, ADD, MAX)
-                nc.sync.dma_start(out[i], result[:])
-            else:
-                nc.scalar.activation(result[:], windows[i][:], RELU, bias=bias[:, 0:1])
-                nc.scalar.dma_start(out[i], result[:])
+            for kb in range(KB):
+                nc.tensor.matmul(
+                    windows[i][:].indirect(offsets[:, i * QC : (i + 1) * QC]),
+                    w_tile[:, kb, :],
+                    x_halves[kb // KH][:, kb % KH, i * Q : (i + 1) * Q],
+                    start=False,
+                    stop=(kb == KB - 1),
+                )
+
+        for i in range(B):
+            for c in range(C):
+                cols = slice(c * (S // C), (c + 1) * (S // C))
+                result = held.tile([P, S // C], F32, name=f"result{i}_{c}")
+                if i % 2 == 0:
+                    nc.vector.tensor_scalar(result[:], windows[i][:, cols], bias[:, 0:1], 0.0, ADD, MAX)
+                    nc.sync.dma_start(out[i][:, cols], result[:])
+                else:
+                    nc.scalar.activation(result[:], windows[i][:, cols], RELU, bias=bias[:, 0:1])
+                    nc.sync.dma_start(out[i][:, cols], result[:])

@@ -25,9 +25,10 @@ def tile_scatter_matmul_kernel(tc, base, x, w, b, offs, out):
         tc.tile_pool(name="held", bufs=1) as held,
         tc.psum_pool(name="banks", bufs=1) as banks,
     ):
-        base_tiles = [held.tile([P, S], BF16, name=f"base{i}") for i in range(B)]
-        for i in range(B):
-            nc.sync.dma_start(base_tiles[i][:], base[i])
+        base_pairs = [held.tile([P, 2, S], BF16, name=f"base_pair{j}") for j in range(B // 2)]
+        for j in range(B // 2):
+            nc.sync.dma_start(base_pairs[j][:], base[2 * j : 2 * j + 2].rearrange("i m t -> m i t"))
+        base_tiles = [base_pairs[i // 2][:, i % 2, :] for i in range(B)]
 
         w_tile = held.tile([P, KB, P], BF16, name="w_tile")
         nc.sync.dma_start(w_tile[:], w.rearrange("(p kb) m -> p kb m", kb=KB))
@@ -55,7 +56,7 @@ def tile_scatter_matmul_kernel(tc, base, x, w, b, offs, out):
 
         windows = [banks.tile([P, S], F32, name=f"window{i}") for i in range(B)]
         for i in range(B):
-            nc.tensor.matmul(windows[i][:], ident[:], base_tiles[i][:], start=True, stop=False)
+            nc.tensor.matmul(windows[i][:], ident[:], base_tiles[i], start=True, stop=False)
 
         for i in range(B):
             for kb in range(KB):

@@ -13,8 +13,6 @@ Q = N // B
 QC = Q // 16
 
 FLOPS = 2 * K * P * N
-G = 2
-KH = KB // G
 C = 2
 WARM = 2
 
@@ -32,13 +30,19 @@ def tile_scatter_matmul_kernel(tc, base, x, w, b, offs, out):
 
         w_tile = held.tile([P, KB, P], BF16, name="w_tile")
         nc.sync.dma_start(w_tile[:], w.rearrange("(p kb) m -> p kb m", kb=KB))
-        x_rows = x.rearrange("(p kb) n -> p kb n", kb=KB)
-        x_halves = [held.tile([P, KH, N], BF16, name=f"x_half{h}") for h in range(G)]
-        nc.sync.dma_start(x_halves[0][:], x_rows[:, 0:KH, :])
 
+        x_rows = x.rearrange("(p kb) n -> p kb n", kb=KB)
+        x_cuts = [(0, KB // 2)] + [(kb, kb + 1) for kb in range(KB // 2, KB)]
+        x_tiles = [held.tile([P, hi - lo, N], BF16, name=f"x_blocks{lo}") for lo, hi in x_cuts]
         offsets = held.tile([P, N // 16], U16, name="offsets")
-        nc.sync.dma_start(offsets[:], offs)
-        nc.sync.dma_start(x_halves[1][:], x_rows[:, KH:KB, :])
+        for (lo, hi), x_tile in zip(x_cuts, x_tiles):
+            nc.sync.dma_start(x_tile[:], x_rows[:, lo:hi, :])
+            if lo == 0:
+                nc.sync.dma_start(offsets[:], offs)
+        x_blocks = [x_tile[:, kb - lo, :] for (lo, hi), x_tile in zip(x_cuts, x_tiles) for kb in range(lo, hi)]
+
+        bias = held.tile([P, 1], F32, name="bias")
+        nc.sync.dma_start(bias[:], b)
 
         zeros = held.tile([P, S], BF16, name="zeros")
         nc.vector.memset(zeros[:], 0.0)
@@ -51,9 +55,6 @@ def tile_scatter_matmul_kernel(tc, base, x, w, b, offs, out):
         ident = held.tile([P, P], BF16, name="ident")
         make_identity(nc, ident[:])
 
-        bias = held.tile([P, 1], F32, name="bias")
-        nc.gpsimd.dma_start(bias[:], b)
-
         windows = [banks.tile([P, S], F32, name=f"window{i}") for i in range(B)]
         for i in range(B):
             nc.tensor.matmul(windows[i][:], ident[:], base_tiles[i], start=True, stop=False)
@@ -63,7 +64,7 @@ def tile_scatter_matmul_kernel(tc, base, x, w, b, offs, out):
                 nc.tensor.matmul(
                     windows[i][:].indirect(offsets[:, i * QC : (i + 1) * QC]),
                     w_tile[:, kb, :],
-                    x_halves[kb // KH][:, kb % KH, i * Q : (i + 1) * Q],
+                    x_blocks[kb][:, i * Q : (i + 1) * Q],
                     start=False,
                     stop=(kb == KB - 1),
                 )

@@ -14,6 +14,7 @@ QC = Q // 16
 
 FLOPS = 2 * K * P * N
 C = 2
+XL = 256
 WARM = 2
 
 
@@ -32,17 +33,15 @@ def tile_scatter_matmul_kernel(tc, base, x, w, b, offs, out):
         nc.sync.dma_start(w_tile[:], w.rearrange("(p kb) m -> p kb m", kb=KB))
 
         x_rows = x.rearrange("(p kb) n -> p kb n", kb=KB)
-        x_cuts = [(0, KB // 2)] + [(kb, kb + 1) for kb in range(KB // 2, KB)]
-        x_tiles = [held.tile([P, hi - lo, N], BF16, name=f"x_blocks{lo}") for lo, hi in x_cuts]
+        x_tile = held.tile([P, KB, N], BF16, name="x_tile")
         offsets = held.tile([P, N // 16], U16, name="offsets")
-        for (lo, hi), x_tile in zip(x_cuts, x_tiles):
-            nc.sync.dma_start(x_tile[:], x_rows[:, lo:hi, :])
-            if lo == 0:
-                nc.sync.dma_start(offsets[:], offs)
-        x_blocks = [x_tile[:, kb - lo, :] for (lo, hi), x_tile in zip(x_cuts, x_tiles) for kb in range(lo, hi)]
-
         bias = held.tile([P, 1], F32, name="bias")
+        nc.sync.dma_start(x_tile[:, 0 : KB // 2, 0:XL], x_rows[:, 0 : KB // 2, 0:XL])
+        nc.sync.dma_start(offsets[:], offs)
+        nc.sync.dma_start(x_tile[:, KB // 2 : KB, 0:XL], x_rows[:, KB // 2 : KB, 0:XL])
         nc.sync.dma_start(bias[:], b)
+        nc.sync.dma_start(x_tile[:, :, XL:N], x_rows[:, :, XL:N])
+        x_blocks = [x_tile[:, kb, :] for kb in range(KB)]
 
         zeros = held.tile([P, S], BF16, name="zeros")
         nc.vector.memset(zeros[:], 0.0)

@@ -14,7 +14,7 @@ QC = Q // 16
 
 FLOPS = 2 * K * P * N
 C = 2
-XL = 256
+XL = 2 * Q
 WARM = 2
 
 

import concourse.mybir as mybir
from concourse.masks import make_identity

BF16, F32, U16 = mybir.dt.bfloat16, mybir.dt.float32, mybir.dt.uint16
RELU = mybir.ActivationFunctionType.Relu
ADD, MAX = mybir.AluOpType.add, mybir.AluOpType.max

P = 128
B, S = 4, 512
K, N = 512, 384
KB = K // P
Q = N // B
QC = Q // 16

FLOPS = 2 * K * P * N
C = 2
XL = 2 * Q
WARM = 2


def tile_scatter_matmul_kernel(tc, base, x, w, b, offs, out):
    nc = tc.nc
    with (
        tc.tile_pool(name="held", bufs=1) as held,
        tc.psum_pool(name="banks", bufs=1) as banks,
    ):
        base_pairs = [held.tile([P, 2, S], BF16, name=f"base_pair{j}") for j in range(B // 2)]
        for j in range(B // 2):
            nc.sync.dma_start(base_pairs[j][:], base[2 * j : 2 * j + 2].rearrange("i m t -> m i t"))
        base_tiles = [base_pairs[i // 2][:, i % 2, :] for i in range(B)]

        w_tile = held.tile([P, KB, P], BF16, name="w_tile")
        nc.sync.dma_start(w_tile[:], w.rearrange("(p kb) m -> p kb m", kb=KB))

        x_rows = x.rearrange("(p kb) n -> p kb n", kb=KB)
        x_tile = held.tile([P, KB, N], BF16, name="x_tile")
        offsets = held.tile([P, N // 16], U16, name="offsets")
        bias = held.tile([P, 1], F32, name="bias")
        nc.sync.dma_start(x_tile[:, 0 : KB // 2, 0:XL], x_rows[:, 0 : KB // 2, 0:XL])
        nc.sync.dma_start(offsets[:], offs)
        nc.sync.dma_start(x_tile[:, KB // 2 : KB, 0:XL], x_rows[:, KB // 2 : KB, 0:XL])
        nc.sync.dma_start(bias[:], b)
        nc.sync.dma_start(x_tile[:, :, XL:N], x_rows[:, :, XL:N])
        x_blocks = [x_tile[:, kb, :] for kb in range(KB)]

        zeros = held.tile([P, S], BF16, name="zeros")
        nc.vector.memset(zeros[:], 0.0)
        unused_bank = banks.tile([P, S], F32, name="unused_bank")
        for r in range(WARM):
            nc.tensor.matmul(unused_bank[:], zeros[:, 0:P], zeros[:], start=True, stop=True)
        unused_relu = held.tile([P, 1], F32, name="unused_relu")
        nc.scalar.activation(unused_relu[:], zeros[:, 0:1], RELU)

        ident = held.tile([P, P], BF16, name="ident")
        make_identity(nc, ident[:])

        windows = [banks.tile([P, S], F32, name=f"window{i}") for i in range(B)]
        for i in range(B):
            nc.tensor.matmul(windows[i][:], ident[:], base_tiles[i], start=True, stop=False)

        for i in range(B):
            for kb in range(KB):
                nc.tensor.matmul(
                    windows[i][:].indirect(offsets[:, i * QC : (i + 1) * QC]),
                    w_tile[:, kb, :],
                    x_blocks[kb][:, i * Q : (i + 1) * Q],
                    start=False,
                    stop=(kb == KB - 1),
                )

        for i in range(B):
            for c in range(C):
                cols = slice(c * (S // C), (c + 1) * (S // C))
                result = held.tile([P, S // C], F32, name=f"result{i}_{c}")
                if i % 2 == 0:
                    nc.vector.tensor_scalar(result[:], windows[i][:, cols], bias[:, 0:1], 0.0, ADD, MAX)
                    nc.sync.dma_start(out[i][:, cols], result[:])
                else:
                    nc.scalar.activation(result[:], windows[i][:, cols], RELU, bias=bias[:, 0:1])
                    nc.sync.dma_start(out[i][:, cols], result[:])
